import numpy as np
import ml_dtypes

BF16 = ml_dtypes.bfloat16


def bf(x):
    return np.asarray(x, np.float32).astype(BF16)


def f32(x):
    return np.asarray(x, np.float32)


def f64(x):
    return np.asarray(x).astype(np.float64)


def striped(idx):
    return np.tile(idx.reshape(-1, 16).T, (8, 1))


S, K, M, N = 512, 128, 512, 192


def setup_inputs():
    return {"base": bf(np.random.standard_normal((M, S))), "x": bf(np.random.standard_normal((K, N))), "w": bf(np.random.standard_normal((K, M)) / np.sqrt(K)), "b": f32(0.5 * np.random.standard_normal((M, 1))), "offs": striped(np.random.permutation(S)[:N])}


def reference(base, x, w, b, offs):
    idx = offs[:16].T.reshape(-1)
    z = f64(base).copy()
    z[:, idx] += f64(w).T @ f64(x)
    return np.tanh(z + f64(b))

@@ -1,0 +1,55 @@
+import concourse.mybir as mybir
+from concourse.masks import make_identity
+
+P = 128
+M, S, K, N = 512, 512, 128, 192
+BLOCKS = M // P
+BF16, F32, U16 = mybir.dt.bfloat16, mybir.dt.float32, mybir.dt.uint16
+TANH = mybir.ActivationFunctionType.Tanh
+
+FLOPS = 2 * M * K * N
+
+
+def tile_scatter_matmul_kernel(tc, base, x, w, b, offs, out):
+    nc = tc.nc
+    with (
+        tc.tile_pool(name="held", bufs=1) as held,
+        tc.tile_pool(name="results", bufs=BLOCKS) as results,
+        tc.psum_pool(name="windows", bufs=BLOCKS) as windows,
+    ):
+        ident = held.tile([P, P], BF16)
+        make_identity(nc, ident[:])
+
+        base_tiles = []
+        for m in range(BLOCKS):
+            base_tile = held.tile([P, S], BF16, name=f"base_tile{m}")
+            nc.sync.dma_start(base_tile[:], base[m * P : (m + 1) * P, :])
+            base_tiles.append(base_tile)
+        weights = held.tile([K, M], BF16)
+        nc.sync.dma_start(weights[:], w)
+        moving = held.tile([K, N], BF16)
+        nc.sync.dma_start(moving[:], x)
+        offsets = held.tile([P, N // 16], U16)
+        nc.sync.dma_start(offsets[:], offs)
+        bias = held.tile([P, BLOCKS], F32)
+        nc.scalar.dma_start(bias[:], b.rearrange("(m p) o -> p (m o)", p=P))
+
+        filled = []
+        for m in range(BLOCKS):
+            window = windows.tile([P, S], F32, name="window")
+            nc.tensor.matmul(window[:], ident[:], base_tiles[m][:], start=True, stop=False)
+            filled.append(window)
+
+        for m in range(BLOCKS):
+            nc.tensor.matmul(
+                filled[m][:].indirect(offsets[:]),
+                weights[:, m * P : (m + 1) * P],
+                moving[:],
+                start=False,
+                stop=True,
+            )
+
+        for m in range(BLOCKS):
+            result = results.tile([P, S], F32, name="result")
+            nc.scalar.activation(result[:], filled[m][:], TANH, bias=bias[:, m : m + 1])
+            nc.sync.dma_start(out[m * P : (m + 1) * P, :], result[:])

@@ -4,6 +4,8 @@ from concourse.masks import make_identity
 P = 128
 M, S, K, N = 512, 512, 128, 192
 BLOCKS = M // P
+HALVES = 2
+WARM_UPS = 3
 BF16, F32, U16 = mybir.dt.bfloat16, mybir.dt.float32, mybir.dt.uint16
 TANH = mybir.ActivationFunctionType.Tanh
 
@@ -16,28 +18,42 @@ def tile_scatter_matmul_kernel(tc, base, x, w, b, offs, out):
         tc.tile_pool(name="held", bufs=1) as held,
         tc.tile_pool(name="results", bufs=BLOCKS) as results,
         tc.psum_pool(name="windows", bufs=BLOCKS) as windows,
+        tc.psum_pool(name="spare", bufs=1) as spare,
     ):
+        zeros = held.tile([P, S], BF16)
+        nc.gpsimd.memset(zeros[:], 0.0)
+
         ident = held.tile([P, P], BF16)
         make_identity(nc, ident[:])
 
-        base_tiles = []
-        for m in range(BLOCKS):
-            base_tile = held.tile([P, S], BF16, name=f"base_tile{m}")
-            nc.sync.dma_start(base_tile[:], base[m * P : (m + 1) * P, :])
-            base_tiles.append(base_tile)
+        bias = held.tile([P, BLOCKS], F32)
+        nc.scalar.dma_start(bias[:], b.rearrange("(m p) o -> p (m o)", p=P))
+
+        table_loaded = held.tile([P, 1], F32)
+        nc.scalar.activation(table_loaded[:], zeros[:, 0:1], TANH)
+
+        idle_bank = spare.tile([P, S], F32)
+        for i in range(WARM_UPS):
+            nc.tensor.matmul(idle_bank[:], zeros[:, 0:P], zeros[:], start=True, stop=True)
+
+        base_blocks = []
+        base_halves = base.rearrange("(h a p) t -> h p a t", h=HALVES, p=P)
+        for h in range(HALVES):
+            base_half = held.tile([P, BLOCKS // HALVES, S], BF16, name=f"base_half{h}")
+            nc.sync.dma_start(base_half[:], base_halves[h])
+            for a in range(BLOCKS // HALVES):
+                base_blocks.append(base_half[:, a, :])
         weights = held.tile([K, M], BF16)
         nc.sync.dma_start(weights[:], w)
         moving = held.tile([K, N], BF16)
         nc.sync.dma_start(moving[:], x)
         offsets = held.tile([P, N // 16], U16)
         nc.sync.dma_start(offsets[:], offs)
-        bias = held.tile([P, BLOCKS], F32)
-        nc.scalar.dma_start(bias[:], b.rearrange("(m p) o -> p (m o)", p=P))
 
         filled = []
         for m in range(BLOCKS):
             window = windows.tile([P, S], F32, name="window")
-            nc.tensor.matmul(window[:], ident[:], base_tiles[m][:], start=True, stop=False)
+            nc.tensor.matmul(window[:], ident[:], base_blocks[m], start=True, stop=False)
             filled.append(window)
 
         for m in range(BLOCKS):

import concourse.mybir as mybir
from concourse.masks import make_identity

P = 128
M, S, K, N = 512, 512, 128, 192
BLOCKS = M // P
HALVES = 2
WARM_UPS = 3
BF16, F32, U16 = mybir.dt.bfloat16, mybir.dt.float32, mybir.dt.uint16
TANH = mybir.ActivationFunctionType.Tanh

FLOPS = 2 * M * K * N


def tile_scatter_matmul_kernel(tc, base, x, w, b, offs, out):
    nc = tc.nc
    with (
        tc.tile_pool(name="held", bufs=1) as held,
        tc.tile_pool(name="results", bufs=BLOCKS) as results,
        tc.psum_pool(name="windows", bufs=BLOCKS) as windows,
        tc.psum_pool(name="spare", bufs=1) as spare,
    ):
        zeros = held.tile([P, S], BF16)
        nc.gpsimd.memset(zeros[:], 0.0)

        ident = held.tile([P, P], BF16)
        make_identity(nc, ident[:])

        bias = held.tile([P, BLOCKS], F32)
        nc.scalar.dma_start(bias[:], b.rearrange("(m p) o -> p (m o)", p=P))

        table_loaded = held.tile([P, 1], F32)
        nc.scalar.activation(table_loaded[:], zeros[:, 0:1], TANH)

        idle_bank = spare.tile([P, S], F32)
        for i in range(WARM_UPS):
            nc.tensor.matmul(idle_bank[:], zeros[:, 0:P], zeros[:], start=True, stop=True)

        base_blocks = []
        base_halves = base.rearrange("(h a p) t -> h p a t", h=HALVES, p=P)
        for h in range(HALVES):
            base_half = held.tile([P, BLOCKS // HALVES, S], BF16, name=f"base_half{h}")
            nc.sync.dma_start(base_half[:], base_halves[h])
            for a in range(BLOCKS // HALVES):
                base_blocks.append(base_half[:, a, :])
        weights = held.tile([K, M], BF16)
        nc.sync.dma_start(weights[:], w)
        moving = held.tile([K, N], BF16)
        nc.sync.dma_start(moving[:], x)
        offsets = held.tile([P, N // 16], U16)
        nc.sync.dma_start(offsets[:], offs)

        filled = []
        for m in range(BLOCKS):
            window = windows.tile([P, S], F32, name="window")
            nc.tensor.matmul(window[:], ident[:], base_blocks[m], start=True, stop=False)
            filled.append(window)

        for m in range(BLOCKS):
            nc.tensor.matmul(
                filled[m][:].indirect(offsets[:]),
                weights[:, m * P : (m + 1) * P],
                moving[:],
                start=False,
                stop=True,
            )

        for m in range(BLOCKS):
            result = results.tile([P, S], F32, name="result")
            nc.scalar.activation(result[:], filled[m][:], TANH, bias=bias[:, m : m + 1])
            nc.sync.dma_start(out[m * P : (m + 1) * P, :], result[:])
